import numpy as np
import ml_dtypes


def mxq(x, axis, fmt="e4m3"):
    dtype, down = {"e4m3": (ml_dtypes.float8_e4m3fn, 7), "e5m2": (ml_dtypes.float8_e5m2, 14)}[fmt]
    v = np.moveaxis(np.asarray(x, np.float32).astype(ml_dtypes.bfloat16).astype(np.float64), axis, -1)
    blocks = v.reshape(v.shape[:-1] + (-1, 32))
    amax = np.abs(blocks).max(-1, keepdims=True)
    byte = np.maximum(np.where(amax > 0, np.frexp(amax)[1] - 1 + 127, 0) - down, 1)
    scale = np.exp2(byte - 127.0)
    codes = (blocks / scale).astype(np.float32).astype(dtype).astype(np.float64)
    return np.moveaxis((codes * scale).reshape(v.shape), -1, axis)


WIDE = False


def mx_kscale(k):
    if not WIDE:
        return np.ones(k)
    levels = np.array([10, -10, 5, -5, 0])
    if k % 512:
        return np.exp2(np.random.permutation(np.resize(levels, k // 32))).repeat(32)
    a = np.empty((k // 512, 16))
    for p in range(k // 512):
        a[p, :8] = np.random.permutation(np.resize(levels, 8))
        for g in range(8):
            far = levels[np.abs(levels - a[p, g]) >= 10]
            a[p, g + 8] = far[np.random.randint(len(far))]
    return np.exp2(a.ravel()).repeat(32)


BF16 = ml_dtypes.bfloat16


def bf(x):
    return np.asarray(x, np.float32).astype(BF16)


def f64(x):
    return np.asarray(x).astype(np.float64)


Y, P, Q, T = 512, 64, 8, 8


def setup_inputs():
    s = mx_kscale(P * Q)
    r = mx_kscale(Y)
    v = mx_kscale(P * T)
    vq = np.repeat(v[::T], Q)
    x = np.random.standard_normal((Y * T, P * Q))
    coil_mix = np.random.standard_normal((P * Q, P * Q)) / (3 * np.sqrt(P * Q))
    line_mix = np.random.standard_normal((Y, Y)) / (3 * np.sqrt(Y))
    con_mix = np.random.standard_normal((P * T, P * T)) / (3 * np.sqrt(P * T))
    return {"x": bf(x * s * np.repeat(r, T)[:, None]),
            "coil_mix": bf(coil_mix / s[:, None] * vq),
            "coil_keep": bf((1 + 0.1 * np.random.standard_normal(P * Q)) / s * vq),
            "line_mix": bf(line_mix / r),
            "line_keep": bf((1 + 0.1 * np.random.standard_normal(Y)) / r),
            "con_mix": bf(con_mix / v[:, None]),
            "con_keep": bf((1 + 0.1 * np.random.standard_normal(P * T)) / v)}


def reference(x, coil_mix, coil_keep, line_mix, line_keep, con_mix, con_keep):
    x = f64(x)
    y = f64(coil_keep) * x + (mxq(x, 1, "e4m3") @ mxq(f64(coil_mix), 0, "e4m3"))
    y = y.reshape(Y, T, P, Q).transpose(0, 3, 2, 1).reshape(Y, Q * P * T)
    z = f64(line_keep)[:, None] * y + (mxq(f64(line_mix), 1, "e4m3") @ mxq(y, 0, "e4m3"))
    z = z.reshape(Y * Q, P * T)
    return f64(con_keep) * z + (mxq(z, 1, "e4m3") @ mxq(f64(con_mix), 0, "e4m3"))

from contextlib import ExitStack

import concourse.mybir as mybir
from concourse.masks import make_identity

F32 = mybir.dt.float32
BF16 = mybir.dt.bfloat16
U32 = mybir.dt.uint32
U8 = mybir.dt.uint8
FP8X4 = mybir.dt.float8_e4m3fn_x4
MULT = mybir.AluOpType.mult
ADD = mybir.AluOpType.add

FLOPS = 3 * 2 * 4096 * 512 * 512

P = 128
ORDER = (
    ("TE", "xtT", 0, 0),
    ("TE", "xtT", 0, 1),
    ("S", "xtC", 0, 0),
    ("S", "xtC", 0, 1),
    ("V", "qx", 0),
    ("V", "coil_turn", 0),
    ("V", "coil_q", 0),
    ("V", "coil_turn", 1),
    ("TE", "s1m", 0, 0),
    ("V", "coil_q", 1),
    ("V", "s1a", 0, 0),
    ("TE", "s1m", 1, 0),
    ("V", "s1a", 1, 0),
    ("TE", "ytT", 0, 0),
    ("V", "coil_turn", 2),
    ("TE", "ytT", 1, 0),
    ("S", "y16", 0, 0),
    ("V", "coil_q", 2),
    ("TE", "con_rowT"),
    ("V", "coil_turn", 3),
    ("S", "y16", 1, 0),
    ("TE", "xtT", 1, 0),
    ("S", "con_rowC"),
    ("S", "y32", 0, 0),
    ("V", "coil_q", 3),
    ("TE", "xtT", 1, 1),
    ("S", "xtC", 1, 0),
    ("TE", "s1m", 2, 0),
    ("S", "xtC", 1, 1),
    ("TE", "s1m", 3, 0),
    ("V", "s1a", 2, 0),
    ("S", "y32", 1, 0),
    ("V", "qx", 1),
    ("TE", "ytT", 2, 0),
    ("V", "s1a", 3, 0),
    ("TE", "s1m", 0, 1),
    ("S", "y16", 2, 0),
    ("TE", "s1m", 1, 1),
    ("V", "s1a", 0, 1),
    ("S", "y32", 2, 0),
    ("TE", "line_T", 0),
    ("V", "s1a", 1, 1),
    ("TE", "ytT", 0, 1),
    ("S", "line_C", 0),
    ("TE", "s1m", 2, 1),
    ("S", "y16", 0, 1),
    ("TE", "line_T", 1),
    ("V", "s1a", 2, 1),
    ("S", "y32", 0, 1),
    ("TE", "ytT", 1, 1),
    ("TE", "s1m", 3, 1),
    ("S", "y16", 1, 1),
    ("TE", "ytT", 2, 1),
    ("V", "s1a", 3, 1),
    ("S", "line_C", 1),
    ("S", "y32", 1, 1),
    ("V", "line_q"),
    ("S", "y16", 2, 1),
    ("TE", "xtT", 2, 0),
    ("S", "y32", 2, 1),
    ("TE", "xtT", 2, 1),
    ("S", "xtC", 2, 0),
    ("TE", "ytT", 3, 0),
    ("TE", "ytT", 3, 1),
    ("S", "xtC", 2, 1),
    ("TE", "xtT", 3, 0),
    ("S", "y16", 3, 0),
    ("V", "qx", 2),
    ("TE", "xtT", 3, 1),
    ("S", "xtC", 3, 0),
    ("TE", "s1m", 0, 2),
    ("S", "xtC", 3, 1),
    ("TE", "s1m", 1, 2),
    ("G", "con_turn", 0),
    ("V", "s1a", 0, 2),
    ("S", "y16", 3, 1),
    ("V", "qx", 3),
    ("TE", "s1m", 2, 2),
    ("S", "y32", 3, 0),
    ("V", "s1a", 1, 2),
    ("G", "con_turn", 1),
    ("S", "y32", 3, 1),
    ("TE", "ytT", 0, 2),
    ("V", "s1a", 2, 2),
    ("TE", "s1m", 0, 3),
    ("G", "con_turn", 2),
    ("S", "y16", 0, 2),
    ("TE", "s1m", 1, 3),
    ("V", "s1a", 0, 3),
    ("TE", "ytT", 1, 2),
    ("S", "y32", 0, 2),
    ("G", "con_turn", 3),
    ("V", "s1a", 1, 3),
    ("TE", "s1m", 2, 3),
    ("S", "y16", 1, 2),
    ("TE", "ytT", 0, 3),
    ("V", "con_q"),
    ("S", "y32", 1, 2),
    ("TE", "s1m", 3, 2),
    ("V", "s1a", 2, 3),
    ("TE", "xtT", 4, 0),
    ("S", "y16", 0, 3),
    ("V", "s1a", 3, 2),
    ("S", "y32", 0, 3),
    ("TE", "xtT", 4, 1),
    ("V", "qy", 0, 0),
    ("S", "xtC", 4, 0),
    ("TE", "ytT", 1, 3),
    ("TE", "s2m", 0, 0, 0),
    ("S", "xtC", 4, 1),
    ("TE", "xtT", 5, 0),
    ("V", "s2a", 0, 0, 0),
    ("S", "y16", 1, 3),
    ("V", "qx", 4),
    ("TE", "xtT", 5, 1),
    ("S", "xtC", 5, 0),
    ("TE", "s2m", 0, 0, 1),
    ("G", "kz", 0, 0, 0),
    ("S", "xtC", 5, 1),
    ("TE", "s1m", 0, 4),
    ("V", "s2a", 0, 0, 1),
    ("TE", "s2m", 0, 0, 2),
    ("S", "y32", 1, 3),
    ("TE", "ytT", 2, 2),
    ("V", "s1a", 0, 4),
    ("S", "z16", 0, 0, 0),
    ("G", "kz", 0, 0, 1),
    ("TE", "s2m", 0, 0, 3),
    ("V", "s2a", 0, 0, 2),
    ("S", "y16", 2, 2),
    ("TE", "ytT", 2, 3),
    ("TE", "s1m", 3, 3),
    ("S", "z16", 0, 0, 1),
    ("V", "qx", 5),
    ("TE", "s1m", 1, 4),
    ("S", "y32", 2, 2),
    ("V", "qy", 1, 0),
    ("S", "y16", 2, 3),
    ("G", "kz", 0, 0, 2),
    ("V", "s1a", 1, 4),
    ("TE", "s2m", 1, 0, 0),
    ("S", "z16", 0, 0, 2),
    ("TE", "ytT", 3, 2),
    ("V", "s2a", 0, 0, 3),
    ("S", "y32", 2, 3),
    ("V", "qy", 2, 0),
    ("TE", "s2m", 1, 0, 1),
    ("S", "y16", 3, 2),
    ("TE", "ytT", 0, 4),
    ("V", "s1a", 3, 3),
    ("G", "kz", 0, 0, 3),
    ("S", "z16", 0, 0, 3),
    ("V", "s2a", 1, 0, 0),
    ("TE", "xtT", 6, 0),
    ("S", "y16", 0, 4),
    ("G", "kz", 1, 0, 0),
    ("TE", "xtT", 6, 1),
    ("V", "s2a", 1, 0, 1),
    ("S", "xtC", 6, 0),
    ("TE", "s1m", 0, 5),
    ("S", "xtC", 6, 1),
    ("TE", "s2m", 1, 0, 2),
    ("V", "s1a", 0, 5),
    ("G", "z16", 1, 0, 0),
    ("S", "z16", 1, 0, 1),
    ("TE", "s2m", 1, 0, 3),
    ("TE", "s1m", 1, 5),
    ("V", "s2a", 1, 0, 2),
    ("S", "y32", 0, 4),
    ("TE", "s1m", 2, 4),
    ("G", "kz", 1, 0, 1),
    ("V", "s1a", 1, 5),
    ("TE", "s2m", 2, 0, 0),
    ("S", "z16", 1, 0, 2),
    ("V", "s1a", 2, 4),
    ("TE", "s1m", 3, 4),
    ("S", "y32", 3, 2),
    ("G", "kz", 1, 0, 2),
    ("V", "s1a", 3, 4),
    ("TE", "ytT", 0, 5),
    ("V", "s2a", 1, 0, 3),
    ("TE", "xtT", 7, 0),
    ("S", "y16", 0, 5),
    ("V", "qx", 6),
    ("TE", "xtT", 7, 1),
    ("S", "xtC", 7, 0),
    ("V", "s2a", 2, 0, 0),
    ("G", "z16", 1, 0, 3),
    ("TE", "s1m", 0, 6),
    ("S", "xtC", 7, 1),
    ("TE", "ytT", 3, 3),
    ("G", "kz", 2, 0, 0),
    ("S", "z16", 2, 0, 0),
    ("TE", "s2m", 2, 0, 1),
    ("S", "y16", 3, 3),
    ("TE", "s2m", 2, 0, 2),
    ("V", "s2a", 2, 0, 1),
    ("TE", "s1m", 1, 6),
    ("G", "kz", 1, 0, 3),
    ("S", "y32", 0, 5),
    ("TE", "s2m", 2, 0, 3),
    ("V", "s2a", 2, 0, 2),
    ("S", "z16", 2, 0, 1),
    ("TE", "ytT", 1, 4),
    ("S", "z16", 2, 0, 2),
    ("V", "qx", 7),
    ("S", "y16", 1, 4),
    ("V", "s1a", 0, 6),
    ("G", "kz", 2, 0, 1),
    ("S", "y32", 3, 3),
    ("V", "s1a", 1, 6),
    ("TE", "s1m", 0, 7),
    ("S", "y32", 1, 4),
    ("TE", "ytT", 0, 6),
    ("V", "qy", 3, 0),
    ("TE", "s1m", 2, 5),
    ("G", "kz", 2, 0, 2),
    ("V", "s1a", 0, 7),
    ("S", "y16", 0, 6),
    ("TE", "ytT", 1, 5),
    ("V", "s2a", 2, 0, 3),
    ("S", "y32", 0, 6),
    ("TE", "s1m", 1, 7),
    ("V", "s1a", 2, 5),
    ("S", "y16", 1, 5),
    ("G", "kz", 2, 0, 3),
    ("TE", "ytT", 0, 7),
    ("S", "z16", 2, 0, 3),
    ("TE", "s1m", 2, 6),
    ("TE", "s2m", 3, 0, 0),
    ("S", "y16", 0, 7),
    ("TE", "s2m", 3, 0, 1),
    ("V", "s2a", 3, 0, 0),
    ("S", "y32", 1, 5),
    ("V", "qy", 0, 1),
    ("S", "y32", 0, 7),
    ("TE", "ytT", 1, 6),
    ("G", "kz", 3, 0, 0),
    ("V", "s2a", 3, 0, 1),
    ("S", "z16", 3, 0, 0),
    ("TE", "ytT", 2, 4),
    ("TE", "s2m", 3, 0, 2),
    ("V", "s1a", 1, 7),
    ("S", "y16", 1, 6),
    ("TE", "s2m", 3, 0, 3),
    ("G", "kz", 3, 0, 1),
    ("V", "s2a", 3, 0, 2),
    ("S", "y16", 2, 4),
    ("TE", "s1m", 3, 5),
    ("S", "y32", 1, 6),
    ("TE", "s2m", 0, 1, 0),
    ("V", "s2a", 3, 0, 3),
    ("S", "y32", 2, 4),
    ("G", "kz", 3, 0, 2),
    ("TE", "ytT", 1, 7),
    ("V", "s2a", 0, 1, 0),
    ("S", "z16", 3, 0, 1),
    ("TE", "s2m", 0, 1, 1),
    ("TE", "s2m", 0, 1, 2),
    ("S", "y16", 1, 7),
    ("V", "s2a", 0, 1, 1),
    ("G", "kz", 3, 0, 3),
    ("TE", "ytT", 2, 5),
    ("S", "z16", 0, 1, 0),
    ("TE", "s2m", 0, 1, 3),
    ("V", "s2a", 0, 1, 2),
    ("S", "y32", 1, 7),
    ("G", "kz", 0, 1, 0),
    ("V", "s2a", 0, 1, 3),
    ("S", "y16", 2, 5),
    ("TE", "ytT", 3, 4),
    ("S", "z16", 0, 1, 1),
    ("V", "s1a", 2, 6),
    ("G", "kz", 0, 1, 1),
    ("S", "y16", 3, 4),
    ("V", "s1a", 3, 5),
    ("TE", "s1m", 2, 7),
    ("S", "y32", 2, 5),
    ("TE", "s1m", 3, 6),
    ("V", "s1a", 2, 7),
    ("G", "kz", 0, 1, 2),
    ("S", "z16", 0, 1, 2),
    ("TE", "ztT", 0, 0),
    ("V", "s1a", 3, 6),
    ("S", "z16", 0, 1, 3),
    ("G", "kz", 0, 1, 3),
    ("TE", "s1m", 3, 7),
    ("S", "ztC", 0, 0),
    ("V", "s1a", 3, 7),
    ("S", "y32", 3, 4),
    ("G", "z16", 3, 0, 2),
    ("S", "z16", 3, 0, 3),
    ("TE", "ztT", 0, 1),
    ("V", "qy", 1, 1),
    ("TE", "ytT", 2, 6),
    ("S", "ztC", 0, 1),
    ("TE", "s2m", 1, 1, 0),
    ("S", "y16", 2, 6),
    ("V", "qz", 0),
    ("TE", "s2m", 1, 1, 1),
    ("TE", "ztT", 1, 0),
    ("S", "y32", 2, 6),
    ("V", "s2a", 1, 1, 0),
    ("TE", "s3m", 0, 0),
    ("S", "ztC", 1, 0),
    ("G", "kz", 1, 1, 0),
    ("V", "s2a", 1, 1, 1),
    ("TE", "s3m", 0, 1),
    ("S", "z16", 1, 1, 0),
    ("TE", "s2m", 1, 1, 2),
    ("V", "s3a", 0, 0),
    ("TE", "ytT", 2, 7),
    ("S", "z16", 1, 1, 1),
    ("G", "kz", 1, 1, 1),
    ("V", "s2a", 1, 1, 2),
    ("TE", "s3m", 0, 2),
    ("S", "y16", 2, 7),
    ("V", "s3a", 0, 1),
    ("TE", "s2m", 1, 1, 3),
    ("TE", "ztT", 1, 1),
    ("S", "z16", 1, 1, 2),
    ("V", "s2a", 1, 1, 3),
    ("G", "kz", 1, 1, 2),
    ("TE", "s3m", 0, 3),
    ("S", "y32", 2, 7),
    ("V", "s3a", 0, 2),
    ("S", "ztC", 1, 1),
    ("TE", "ytT", 3, 5),
    ("V", "qy", 2, 1),
    ("S", "z16", 1, 1, 3),
    ("TE", "ytT", 3, 6),
    ("G", "kz", 1, 1, 3),
    ("V", "s3a", 0, 3),
    ("TE", "s2m", 2, 1, 0),
    ("S", "y16", 3, 5),
    ("TE", "s2m", 2, 1, 1),
    ("V", "s2a", 2, 1, 0),
    ("S", "y16", 3, 6),
    ("V", "qz", 1),
    ("TE", "s2m", 2, 1, 2),
    ("S", "z16", 2, 1, 0),
    ("G", "kz", 2, 1, 0),
    ("V", "s2a", 2, 1, 1),
    ("S", "y32", 3, 5),
    ("TE", "s3m", 1, 0),
    ("TE", "s3m", 1, 1),
    ("V", "s3a", 1, 0),
    ("S", "z16", 2, 1, 1),
    ("TE", "ztT", 2, 0),
    ("V", "s2a", 2, 1, 2),
    ("G", "kz", 2, 1, 1),
    ("S", "y32", 3, 6),
    ("TE", "s3m", 1, 2),
    ("V", "s3a", 1, 1),
    ("S", "ztC", 2, 0),
    ("TE", "ztT", 2, 1),
    ("G", "kz", 2, 1, 2),
    ("S", "z16", 2, 1, 2),
    ("V", "s3a", 1, 2),
    ("TE", "s3m", 1, 3),
    ("S", "ztC", 2, 1),
    ("TE", "ytT", 3, 7),
    ("V", "s3a", 1, 3),
    ("TE", "s2m", 2, 1, 3),
    ("S", "y16", 3, 7),
    ("V", "qz", 2),
    ("S", "y32", 3, 7),
    ("V", "qy", 3, 1),
    ("TE", "s3m", 2, 0),
    ("TE", "s3m", 2, 1),
    ("V", "s2a", 2, 1, 3),
    ("TE", "ztT", 3, 0),
    ("V", "s3a", 2, 0),
    ("S", "z16", 2, 1, 3),
    ("G", "kz", 2, 1, 3),
    ("TE", "ztT", 3, 1),
    ("S", "ztC", 3, 0),
    ("V", "s3a", 2, 1),
    ("TE", "s3m", 2, 2),
    ("S", "ztC", 3, 1),
    ("TE", "s3m", 2, 3),
    ("V", "s3a", 2, 2),
    ("TE", "s2m", 3, 1, 0),
    ("TE", "s2m", 3, 1, 1),
    ("V", "qz", 3),
    ("TE", "ztT", 4, 0),
    ("V", "s2a", 3, 1, 0),
    ("TE", "s3m", 3, 0),
    ("S", "ztC", 4, 0),
    ("V", "s3a", 2, 3),
    ("G", "kz", 3, 1, 0),
    ("TE", "s2m", 3, 1, 2),
    ("S", "z16", 3, 1, 0),
    ("V", "s2a", 3, 1, 1),
    ("TE", "s3m", 3, 1),
    ("TE", "ztT", 4, 1),
    ("V", "s3a", 3, 0),
    ("S", "z16", 3, 1, 1),
    ("G", "kz", 3, 1, 1),
    ("V", "s2a", 3, 1, 2),
    ("TE", "s3m", 3, 2),
    ("S", "ztC", 4, 1),
    ("TE", "ztT", 6, 0),
    ("V", "s3a", 3, 1),
    ("S", "z16", 3, 1, 2),
    ("G", "kz", 3, 1, 2),
    ("TE", "s3m", 3, 3),
    ("V", "s3a", 3, 2),
    ("S", "ztC", 6, 0),
    ("TE", "s2m", 3, 1, 3),
    ("TE", "ztT", 5, 0),
    ("V", "qz", 4),
    ("V", "s2a", 3, 1, 3),
    ("TE", "s3m", 4, 0),
    ("S", "ztC", 5, 0),
    ("TE", "ztT", 5, 1),
    ("V", "s3a", 3, 3),
    ("G", "kz", 3, 1, 3),
    ("S", "z16", 3, 1, 3),
    ("V", "s3a", 4, 0),
    ("TE", "s3m", 4, 1),
    ("S", "ztC", 5, 1),
    ("TE", "ztT", 6, 1),
    ("V", "s3a", 4, 1),
    ("TE", "s3m", 4, 2),
    ("V", "qz", 5),
    ("S", "ztC", 6, 1),
    ("TE", "s3m", 4, 3),
    ("V", "s3a", 4, 2),
    ("TE", "ztT", 7, 0),
    ("V", "qz", 6),
    ("TE", "s3m", 5, 0),
    ("S", "ztC", 7, 0),
    ("TE", "ztT", 7, 1),
    ("V", "s3a", 4, 3),
    ("V", "s3a", 5, 0),
    ("TE", "s3m", 5, 1),
    ("S", "ztC", 7, 1),
    ("TE", "s3m", 5, 2),
    ("V", "s3a", 5, 1),
    ("V", "qz", 7),
    ("TE", "s3m", 5, 3),
    ("V", "s3a", 5, 2),
    ("TE", "s3m", 6, 0),
    ("V", "s3a", 5, 3),
    ("V", "s3a", 6, 0),
    ("TE", "s3m", 6, 1),
    ("TE", "s3m", 6, 2),
    ("V", "s3a", 6, 1),
    ("TE", "s3m", 6, 3),
    ("V", "s3a", 6, 2),
    ("TE", "s3m", 7, 0),
    ("V", "s3a", 6, 3),
    ("V", "s3a", 7, 0),
    ("TE", "s3m", 7, 1),
    ("TE", "s3m", 7, 2),
    ("V", "s3a", 7, 1),
    ("TE", "s3m", 7, 3),
    ("V", "s3a", 7, 2),
    ("V", "s3a", 7, 3),
)
BUFS = {"x": 2, "xg": 3, "xq": 4, "y32c": 6, "y32l": 4, "gq": 4, "q": 3, "z32": 2, "kz": 4}


def tile_coil_line_contrast_residual_t1_kernel(
    tc, x, coil_mix, coil_keep, line_mix, line_keep, con_mix, con_keep, out
):
    nc = tc.nc
    x_v = x.rearrange("(p t c) k -> p t c k", t=4, c=8)
    out_v = out.rearrange("(p t q) n -> p t q n", t=4, q=8)

    with ExitStack() as ctx:
        keep = ctx.enter_context(tc.tile_pool(name="keep", bufs=1))
        pool = ctx.enter_context(tc.tile_pool(name="pool", bufs=2))
        psum = ctx.enter_context(tc.psum_pool(name="psum", bufs=2))
        ctx.enter_context(tc.manual_schedule())

        def big(shape, dtype, tag):
            return pool.tile(shape, dtype, name=tag, tag=tag, bufs=BUFS[tag], align_bytes=64)

        def bank(shape, tag):
            return psum.tile(shape, F32, name=tag, tag=tag, bufs=2)

        def fixed(shape, dtype, name):
            return keep.tile(shape, dtype, name=name, tag=name, bufs=1, align_bytes=64)

        def pack(width):
            q = big([P, width], U32, "q")
            s = pool.tile([P, width], U8, name="qs", tag="qs", bufs=BUFS["q"], align_bytes=64)
            return q, s

        def quantize(pair, grouped, lo, hi):
            nc.vector.quantize_mx(
                out=pair[0][:, lo:hi].bitcast(FP8X4),
                scales=pair[1][:, lo:hi],
                in_=grouped[:, 4 * lo : 4 * hi],
            )

        def mm(dst, st, s0, mv):
            nc.tensor.matmul_mx(
                out=dst[:],
                lhsT=st[0][:, s0 : s0 + P].bitcast(FP8X4),
                lhsT_scale=st[1][:, s0 : s0 + P],
                rhs=mv[0][:].bitcast(FP8X4),
                rhs_scale=mv[1][:],
                start=True,
                stop=True,
            )

        def turn_t(src_words, tag):
            b = bank([P, 2, 2, P], tag)
            for i in range(2):
                for u in range(2):
                    nc.tensor.transpose(b[:, i, u, :], src_words[i][:, u::2], ident[:])
            return b

        def turn_c(b, dst, engine):
            o = dst.bitcast(F32).rearrange("p (t r u) -> p t r u", t=2, u=2)
            v = b[:].rearrange("p t u r -> p t r u")
            if engine == "S":
                nc.scalar.copy(out=o, in_=v)
            else:
                nc.vector.tensor_copy(out=o, in_=v)

        def cpy(e, out, in_):
            if e == "S":
                nc.scalar.copy(out=out, in_=in_)
            else:
                nc.vector.tensor_copy(out=out, in_=in_)

        tb = {}

        coil_raw = big([P, 4, 512], BF16, "gq")
        line_raw = big([P, 4, 512], BF16, "gq")
        con_raw = big([P, 4, 512], BF16, "z32")
        x_c = []
        vecs = fixed([P, 3, 16], BF16, "vecs")

        def load_pair(i):
            xp = big([P, 4, 2, 512], BF16, "x")
            if i == 0:
                nc.sync.dma_start(out=xp[:, :, 0, :], in_=x_v[:, :, 0, :])
                nc.sync.dma_start(out=coil_raw[:], in_=coil_mix.rearrange("(p j) c -> p j c", j=4))
                nc.sync.dma_start(out=xp[:, :, 1, :], in_=x_v[:, :, 1, :])
                nc.scalar.dma_start(out=vecs[:, 0, 0:4], in_=coil_keep.rearrange("(p t) -> p t", t=4))
                nc.scalar.dma_start(out=vecs[:, 1, 0:4], in_=line_keep.rearrange("(p t) -> p t", t=4))
                nc.scalar.dma_start(out=vecs[:, 2, 0:4], in_=con_keep.rearrange("(p t) -> p t", t=4))
                nc.sync.dma_start(out=line_raw[:], in_=line_mix.rearrange("(p t) k -> p t k", t=4))
            else:
                nc.sync.dma_start(out=xp[:], in_=x_v[:, :, 2 * i : 2 * i + 2, :])
            if i == 1:
                con_v = con_mix.rearrange("(b j c) w -> c b j w", j=4, c=8)
                for c in range(8):
                    nc.sync.dma_start(out=con_raw[c:P:8, :, :], in_=con_v[c])
            x_c.append((xp, 0))
            x_c.append((xp, 1))

        ident = fixed([P, P], F32, "ident")
        make_identity(nc, ident[:])

        codes = {}
        for name in ("coil", "line", "con"):
            codes[name] = (fixed([P, 512], U32, name + "_q"), fixed([P, 512], U8, name + "_s"))

        xg = {}
        xq = {}
        ps1 = {}
        ps2 = {}
        ps3 = {}
        y32c = {}
        y32l = {}
        yg = {}
        yq = {}
        z32 = {}
        zg = {}
        zq = {}
        kz = {}
        z16 = fixed([P, 4, 4, 2, 512], BF16, "z16")
        con_b = fixed([P, 512], F32, "con_b")

        def xtT(e, c, b):
            if b == 0:
                xg[c] = big([P, 2048], BF16, "xg")
            src, off = x_c[c]
            words = [src[:, 2 * b + i, off, :].bitcast(F32) for i in range(2)]
            tb["x", c, b] = turn_t(words, "ps3")

        def xtC(e, c, b):
            turn_c(tb["x", c, b], xg[c][:, 1024 * b : 1024 * (b + 1)], e)

        def qx(e, c):
            q = big([P, 512], U32, "xq")
            s = pool.tile([P, 512], U8, name="xs", tag="xs", bufs=BUFS["xq"], align_bytes=64)
            xq[c] = (q, s)
            quantize(xq[c], xg[c], 0, 512)

        def s1m(e, g, c):
            ps1[g, c] = bank([P, 512], "ps1")
            mm(ps1[g, c], codes["coil"], g * P, xq[c])

        def s1a(e, g, c):
            y32c[g, c] = big([P, 512], F32, "y32c")
            xk = xg[c][:].rearrange("p (r e) -> p r e", e=4)[:, :, g]
            nc.vector.scalar_tensor_tensor(
                out=y32c[g, c][:], in0=xk, scalar=vecs[:, 0, g : g + 1], in1=ps1[g, c][:], op0=MULT, op1=ADD
            )

        def ytT(e, g, c):
            u = (g, c // 4)
            k = c % 4
            if k == 0:
                y32l[u] = big([P, 4, 512], F32, "y32l")
                yg[u] = big([P, 2048], BF16, "gq")
            b = bank([P, 4, P], "tr")
            for t in range(4):
                nc.tensor.transpose(b[:, t, :], y32c[g, c][:, t * P : (t + 1) * P], ident[:])
            tb["y", g, c] = b

        def y16(e, g, c):
            u, k, b = (g, c // 4), c % 4, tb["y", g, c]
            cpy(
                e,
                out=yg[u][:, 512 * k : 512 * (k + 1)].rearrange("p (f s t) -> p f s t", f=2, t=4),
                in_=b[:].rearrange("p t (s f) -> p f s t", f=2),
            )

        def y32(e, g, c):
            u, k, b = (g, c // 4), c % 4, tb["y", g, c]
            cpy(
                e,
                out=y32l[u][:, :, P * k : P * (k + 1)].rearrange("p t (f s) -> p t f s", f=2),
                in_=b[:].rearrange("p t (s f) -> p t f s", f=2),
            )

        def qy(e, g, h):
            yq[g, h] = pack(512)
            quantize(yq[g, h], yg[g, h], 0, 512)

        def s2m(e, g, h, m):
            ps2[g, h, m] = bank([P, 512], "ps2")
            mm(ps2[g, h, m], codes["line"], m * P, yq[g, h])

        def s2a(e, g, h, m):
            if m == 0:
                z32[g, h] = big([P, 4, 512], F32, "z32")
            nc.vector.scalar_tensor_tensor(
                out=z32[g, h][:, m, :],
                in0=y32l[g, h][:, m, :],
                scalar=vecs[:, 1, m : m + 1],
                in1=ps2[g, h, m][:],
                op0=MULT,
                op1=ADD,
            )

        def z16p(e, g, h, t):
            dst = z16[:, g, t, :, :].rearrange("p f (b c j) -> p (f b) c j", c=8, j=4)
            dst = dst[:, :, 4 * h : 4 * h + 4, :]
            src = z32[g, h][:, t, :].rearrange("p (c n j) -> p n c j", c=4, j=4)
            if e == "G":
                nc.gpsimd.tensor_scalar(out=dst, in0=src, scalar1=1.0, scalar2=0.0, op0=MULT, op1=ADD)
            else:
                nc.scalar.copy(out=dst, in_=src)

        def kzp(e, g, h, t):
            if h == 0 and t == 0:
                kz[g] = big([P, 4, 2, 512], F32, "kz")
            con_h = con_b[:].rearrange("p (o s c) -> p o s c", o=1, c=8)[:, :, :, 4 * h : 4 * h + 4]
            nc.gpsimd.tensor_tensor(
                out=kz[g][:, t, :, :].rearrange("p f (s c) -> p f s c", c=8)[:, :, :, 4 * h : 4 * h + 4],
                in0=z32[g, h][:, t, :].rearrange("p (c f s) -> p f s c", c=4, f=2),
                in1=con_h.to_broadcast([P, 2, 64, 4]),
                op=MULT,
            )

        def ztT(e, i, b):
            g, f = i // 2, i % 2
            if b == 0:
                zg[i] = big([P, 2048], BF16, "gq")
            words = [z16[:, g, 2 * b + k, f, :].bitcast(F32) for k in range(2)]
            tb["z", i, b] = turn_t(words, "tr")

        def ztC(e, i, b):
            turn_c(tb["z", i, b], zg[i][:, 1024 * b : 1024 * (b + 1)], e)

        def qz(e, i):
            zq[i] = pack(512)
            quantize(zq[i], zg[i], 0, 512)

        def s3m(e, i, t):
            ps3[i, t] = bank([P, 512], "ps3")
            mm(ps3[i, t], zq[i], t * P, codes["con"])

        def s3a(e, i, t):
            g, f = i // 2, i % 2
            o = kz[g][:, t, f, :]
            nc.vector.tensor_tensor(out=o, in0=ps3[i, t][:], in1=o, op=ADD)
            coil = g + 4 * f
            if i == 7:
                nc.sync.dma_start(out=out_v[:, t, coil, :], in_=o)
            elif t == 3:
                nc.sync.dma_start(out=out_v[:, :, coil, :], in_=kz[g][:, :, f, :])

        prep = {}

        def line_T(e, b):
            if b == 0:
                prep["line"] = big([P, 2048], BF16, "gq")
            words = [line_raw[:, 2 * b + k, :].bitcast(F32) for k in range(2)]
            tb["l", b] = turn_t(words, "ps2")

        def line_C(e, b):
            turn_c(tb["l", b], prep["line"][:, 1024 * b : 1024 * (b + 1)], e)

        def line_q(e):
            quantize(codes["line"], prep["line"], 0, 512)

        def con_turn(e, part):
            if part == 0:
                prep["con"] = fixed([P, 2048], BF16, "con_g")
            lo, hi = 128 * part, 128 * (part + 1)
            nc.gpsimd.tensor_scalar(
                out=prep["con"][:, 4 * lo : 4 * hi].rearrange("p (w j) -> p w j", j=4),
                in0=con_raw[:, :, lo:hi].rearrange("p j w -> p w j"),
                scalar1=1.0,
                scalar2=0.0,
                op0=MULT,
                op1=ADD,
            )

        def con_q(e):
            quantize(codes["con"], prep["con"], 0, 512)

        def con_rowT(e):
            v32 = fixed([P, 4], F32, "v32")
            nc.gpsimd.tensor_copy(out=v32[:], in_=vecs[:, 2, 0:4])
            bc = bank([P, 4, P], "ps2")
            for e in range(4):
                nc.tensor.transpose(bc[:, e, :], v32[:, e : e + 1].to_broadcast([P, P]), ident[:])
            tb["con"] = bc

        def con_rowC(e):
            bc = tb["con"]
            nc.scalar.copy(
                out=con_b[:].rearrange("p (r e) -> p r e", e=4), in_=bc[:].rearrange("p e r -> p r e")
            )

        def coil_turn(e, g):
            if g == 0:
                prep["coil"] = big([P, 2048], BF16, "gq")
            nc.vector.tensor_copy(
                out=prep["coil"][:, 512 * g : 512 * (g + 1)].rearrange("p (m j) -> p m j", j=4),
                in_=coil_raw[:].rearrange("p j (m t) -> p t m j", t=4)[:, g, :, :],
            )

        def coil_q(e, g):
            quantize(codes["coil"], prep["coil"], P * g, P * (g + 1))

        for i in range(4):
            load_pair(i)
        fns = {
            "xtT": xtT, "xtC": xtC, "qx": qx, "s1m": s1m, "s1a": s1a, "ytT": ytT, "y16": y16, "y32": y32,
            "qy": qy, "s2m": s2m, "s2a": s2a, "z16": z16p, "kz": kzp, "ztT": ztT, "ztC": ztC, "qz": qz,
            "s3m": s3m, "s3a": s3a, "line_T": line_T, "line_C": line_C, "line_q": line_q,
            "con_turn": con_turn, "con_q": con_q, "con_rowT": con_rowT, "con_rowC": con_rowC,
            "coil_turn": coil_turn, "coil_q": coil_q,
        }
        for e, name, *args in ORDER:
            fns[name](e, *args)
